import numpy as np
import ml_dtypes


def mxq(x, axis, fmt="e4m3"):
    dtype, down = {"e4m3": (ml_dtypes.float8_e4m3fn, 7), "e5m2": (ml_dtypes.float8_e5m2, 14)}[fmt]
    v = np.moveaxis(np.asarray(x, np.float32).astype(ml_dtypes.bfloat16).astype(np.float64), axis, -1)
    blocks = v.reshape(v.shape[:-1] + (-1, 32))
    amax = np.abs(blocks).max(-1, keepdims=True)
    byte = np.maximum(np.where(amax > 0, np.frexp(amax)[1] - 1 + 127, 0) - down, 1)
    scale = np.exp2(byte - 127.0)
    codes = (blocks / scale).astype(np.float32).astype(dtype).astype(np.float64)
    return np.moveaxis((codes * scale).reshape(v.shape), -1, axis)


WIDE = False


def mx_kscale(k):
    if not WIDE:
        return np.ones(k)
    levels = np.array([10, -10, 5, -5, 0])
    if k % 512:
        return np.exp2(np.random.permutation(np.resize(levels, k // 32))).repeat(32)
    a = np.empty((k // 512, 16))
    for p in range(k // 512):
        a[p, :8] = np.random.permutation(np.resize(levels, 8))
        for g in range(8):
            far = levels[np.abs(levels - a[p, g]) >= 10]
            a[p, g + 8] = far[np.random.randint(len(far))]
    return np.exp2(a.ravel()).repeat(32)


def f64(x):
    return np.asarray(x).astype(np.float64)


def striped(idx):
    return np.tile(idx.reshape(-1, 16).T, (8, 1)).astype(np.uint16)


def unstriped(offs):
    return offs[:16].T.reshape(-1).astype(np.int64)


E2M1 = np.array([0.0, 0.5, 1.0, 1.5, 2.0, 3.0, 4.0, 6.0, -0.0, -0.5, -1.0, -1.5, -2.0, -3.0, -4.0, -6.0])


def pack_weight(w, fmt):
    k, n = w.shape
    w = f64(np.asarray(w, np.float32).astype(ml_dtypes.bfloat16)).reshape(k // 32, 32, n)
    amax = np.abs(w).max(1)
    if fmt == "e4m3":
        byte = np.frexp(amax)[1] - 1 + 127 - 7
    else:
        mant, ex = np.frexp(amax / 6.0)
        byte = np.where(mant > 0.5, ex, ex - 1) + 127
    byte = np.clip(np.where(amax > 0, byte, 1), 1, 254)
    scaled = (w * np.exp2(127.0 - byte)[:, None, :]).reshape(k, n).astype(np.float32)
    by_word = np.ascontiguousarray(scaled.reshape(k // 512, 128, 4, n).transpose(0, 1, 3, 2))
    if fmt == "e4m3":
        words = by_word.astype(ml_dtypes.float8_e4m3fn).view(np.uint8)
    else:
        c = by_word.astype(ml_dtypes.float4_e2m1fn).view(np.uint8) & 0xF
        words = (c[..., 0::2] | (c[..., 1::2] << 4)).reshape(k // 512, 128, 2 * n)
    return np.ascontiguousarray(words), np.ascontiguousarray(byte.astype(np.uint8).reshape(k // 512, 16, n))


def unpack_weight(words, scales, fmt):
    g, _, n = scales.shape
    words = np.ascontiguousarray(words).reshape(g, 128, n, -1)
    if fmt == "e4m3":
        vals = words.view(ml_dtypes.float8_e4m3fn).astype(np.float64)
    else:
        nib = np.empty((g, 128, n, 4), np.uint8)
        nib[..., 0::2] = words & 0xF
        nib[..., 1::2] = words >> 4
        vals = E2M1[nib]
    vals = vals * np.repeat(np.exp2(scales.astype(np.float64) - 127.0), 8, axis=1)[..., None]
    return vals.transpose(0, 1, 3, 2).reshape(g * 512, n)


def gelu(v):
    return 0.5 * v * (1.0 + np.tanh(np.sqrt(2.0 / np.pi) * (v + 0.044715 * v**3)))


K, KA, H, T, S, T2, P = 1536, 1024, 1024, 4096, 1024, 2048, 512

def setup_inputs():
    n = np.random.standard_normal
    s = mx_kscale(K)[:, None]
    u = mx_kscale(H)[:, None]
    tab_words, tab_scales = pack_weight(n((K, T)) * s, "e4m3")
    w4_words, w4_scales = pack_weight(1.5 * n((KA, H)) / np.sqrt(K) / s[:KA], "e2m1")
    return {
        "tab_words": tab_words, "tab_scales": tab_scales,
        "w4_words": w4_words, "w4_scales": w4_scales,
        "w1": (1.5 * n((K - KA, H)) / np.sqrt(K) / s[KA:]).astype(np.float32),
        "ex": (0.5 * np.exp(0.3 * n((H, S))) * u).astype(np.float32),
        "page0": (n((H, T2)) * u).astype(np.float32),
        "wgs": np.exp(0.3 * n((128, S))).astype(np.float32),
        "rd": (n(H) / np.sqrt(H) / u[:, 0] ** 2).astype(np.float32),
        "pair": n((P, P)).astype(np.float32),
        "gz": np.exp(0.4 * n(P)).astype(np.float32),
        "offs": striped(np.random.permutation(T)[:S]),
        "offs2": striped(np.random.permutation(T2)[:S]),
        "offs3": striped(np.random.permutation(T2)[:P]),
        "offs4": striped(np.random.permutation(T2)[:P]),
    }

def reference(tab_words, tab_scales, w4_words, w4_scales, w1, ex, page0, wgs, rd, pair, gz, offs, offs2, offs3, offs4):
    v = unpack_weight(tab_words, tab_scales, "e4m3")[:, unstriped(offs)]
    w4 = unpack_weight(w4_words, w4_scales, "e2m1")
    d = w4.T @ v[:KA] + mxq(f64(w1), 0, "e4m3").T @ v[KA:]
    bend = 0.5 * d * (1.0 + np.tanh(0.7978845608 * (d + 0.044715 * d ** 3)))
    h = (d + bend) * f64(ex)
    page = f64(page0).copy()
    page[:, unstriped(offs2)] = np.tile(f64(wgs), (H // 128, 1)) * h
    x1 = page[:, unstriped(offs3)]
    x2 = np.abs(page[:, unstriped(offs4)]) * f64(rd)[:, None]
    e = mxq(x1, 0, "e4m3").T @ mxq(x2, 0, "e4m3")
    return np.maximum(e, f64(pair)) * f64(gz)[:, None]

@@ -1,0 +1,348 @@
+from contextlib import ExitStack
+
+import concourse.mybir as mybir
+from concourse.masks import make_identity
+
+K, KA, H, T, S, T2, NP = 1536, 1024, 1024, 4096, 1024, 2048, 512
+FLOPS = 2 * K * H * S + 2 * H * NP * NP
+
+F32 = mybir.dt.float32
+BF16 = mybir.dt.bfloat16
+I32 = mybir.dt.int32
+U32 = mybir.dt.uint32
+U16 = mybir.dt.uint16
+U8 = mybir.dt.uint8
+FP8X4 = mybir.dt.float8_e4m3fn_x4
+FP4X4 = mybir.dt.float4_e2m1fn_x4
+ACT = mybir.ActivationFunctionType
+ALU = mybir.AluOpType
+
+P = 128
+KB = 1024
+MODE = "Q"
+
+
+def woven(dst, src):
+    return (
+        dst.rearrange("p (c i t) -> p c t i", i=4, t=4),
+        src.rearrange("p t (c i) -> p c t i", i=4),
+    )
+
+
+def tile_list_gauze_ageing_match_kernel(
+    tc, tab_words, tab_scales, w4_words, w4_scales, w1, ex, page0, wgs, rd, pair, gz,
+    offs, offs2, offs3, offs4, out,
+):
+    nc = tc.nc
+    with ExitStack() as ctx:
+        lists = ctx.enter_context(tc.tile_pool(name="lists", bufs=1))
+        keep = ctx.enter_context(tc.tile_pool(name="keep", bufs=1))
+        shared = ctx.enter_context(tc.tile_pool(name="shared", bufs=1))
+        psum = ctx.enter_context(tc.psum_pool(name="psum", bufs=1))
+
+        def placed(name, shape, dtype, kb):
+            return shared.tile(shape, dtype, name=name, offset=kb * KB, align_bytes=64)
+
+        def kept(name, shape, dtype, bufs=1):
+            return keep.tile(shape, dtype, name=name, bufs=bufs, align_bytes=64)
+
+        idx = lists.tile([P, S // 16], U16, name="idx")
+        idx2 = lists.tile([P, S // 16], U16, name="idx2")
+        idx3 = lists.tile([P, NP // 16], U16, name="idx3")
+        idx4 = lists.tile([P, NP // 16], U16, name="idx4")
+
+        scale_window = placed("scale_window", [P, T], U8, 70)
+        nc.vector.memset(scale_window[:].bitcast(I32), 0)
+        w4_planes = kept("w4_planes", [P, 2, H], U8)
+        shifted_scales = kept("shifted_scales", [P, S], U8)
+
+        nc.sync.dma_start(idx[:], offs)
+
+        for q in range(4):
+            nc.gpsimd.dma_start(
+                out=scale_window[32 * q : 32 * q + 12, :].bitcast(I32),
+                in_=tab_scales[:, 4 * q : 4 * q + 4, :].bitcast(I32),
+            )
+        table = [placed("table%d" % a, [P, T], I32, 16 * a) for a in range(3)]
+
+        def load_table(a):
+            nc.sync.dma_start(
+                out=table[a][:], in_=tab_words[a].rearrange("p n i -> p (n i)").bitcast(I32)
+            )
+
+        w4_codes = [kept("w4_codes%d" % b, [P, 2, 2 * 512], U8) for b in range(2)]
+        w1_codes = [kept("w1_codes%d" % b, [P, 512], U32) for b in range(2)]
+        w1_plane = [kept("w1_plane%d" % b, [P, 512], U8) for b in range(2)]
+        w1_raw = {}
+
+        def load_weights(b):
+            nc.sync.dma_start(
+                out=w4_codes[b][:].bitcast(I32),
+                in_=w4_words.rearrange("a p c -> p a c")[:, :, 1024 * b : 1024 * (b + 1)].bitcast(I32),
+            )
+            w1_raw[b] = placed("w1_raw%d" % b, [P, 4, 512], F32, 52)
+            nc.sync.dma_start(
+                out=w1_raw[b][:],
+                in_=w1[:, 512 * b : 512 * (b + 1)].rearrange("(p i) c -> p i c", i=4),
+            )
+
+        def quantize_w1(b):
+            rounded = placed("w1_rounded%d" % b, [P, 2048], BF16, 60 if b == 0 else 76)
+            dst, src = woven(rounded[:], w1_raw[b][:])
+            nc.scalar.copy(out=dst, in_=src)
+            nc.vector.quantize_mx(
+                out=w1_codes[b][:].bitcast(FP8X4), scales=w1_plane[b][:], in_=rounded[:]
+            )
+
+        load_table(0)
+        load_weights(0)
+        for q in range(4):
+            nc.sync.dma_start(
+                out=w4_planes[32 * q : 32 * q + 4, :, :].bitcast(I32),
+                in_=w4_scales[:, 4 * q : 4 * q + 4, :].rearrange("a r c -> r a c").bitcast(I32),
+            )
+        nc.sync.dma_start(idx2[:], offs2)
+        load_table(1)
+        load_table(2)
+
+        picked_scales = kept("picked_scales", [P, S], U8)
+        nc.vector.tensor_copy(picked_scales[:], scale_window[:].indirect(idx[:]))
+        nc.gpsimd.dma_start(
+            out=shifted_scales[0:112, :].bitcast(I32), in_=picked_scales[4:116, :].bitcast(I32)
+        )
+        v_plane = [picked_scales[:], shifted_scales[:], picked_scales[8:P, :]]
+        identity = kept("identity", [P, P], F32)
+        make_identity(nc, identity[:])
+
+        v_codes = [placed("v_codes%d" % a, [P, S], U32, 64 + 4 * a) for a in range(3)]
+        nc.vector.tensor_copy(v_codes[0][:], table[0][:].bitcast(U32).indirect(idx[:]))
+        quantize_w1(0)
+        nc.vector.tensor_copy(v_codes[1][:], table[1][:].bitcast(U32).indirect(idx[:]))
+        for half in range(2):
+            nc.vector.tensor_copy(
+                v_codes[2][:, 512 * half : 512 * (half + 1)],
+                table[2][:].bitcast(U32).indirect(idx[:, 32 * half : 32 * (half + 1)]),
+            )
+
+        exposure, page = {}, {}
+
+        def rows_of(x, n):
+            b, t = divmod(n, 4)
+            return x[512 * b : 512 * (b + 1), :].rearrange("(p t) j -> p t j", t=4)[:, t, :]
+
+        def load_exposure(n):
+            exposure[n] = placed("exposure%d" % n, [P, S], F32, 76 + 4 * (n % 4))
+            nc.sync.dma_start(out=exposure[n][:], in_=rows_of(ex, n))
+
+        def load_page(n):
+            if n < 2:
+                page[n] = kept("page%d" % n, [P, T2], F32)
+            else:
+                page[n] = placed("page%d" % n, [P, T2], F32, 8 * (n - 2))
+            nc.sync.dma_start(out=page[n][:], in_=rows_of(page0, n))
+
+        wgs_first = kept("wgs_first", [P, S], F32)
+        wgs_rest = kept("wgs_rest", [P, 3, S], F32)
+        wgs_rows = wgs.rearrange("(q t) j -> q t j", t=4)
+        weight = [wgs_first[:]] + [wgs_rest[:, t, :] for t in range(3)]
+
+        load_exposure(0)
+        for q in (0, 2, 1, 3):
+            nc.sync.dma_start(out=wgs_first[32 * q : 32 * q + 32, :], in_=wgs_rows[:, 0, :])
+        load_page(0)
+        nc.sync.dma_start(idx3[:], offs3)
+        nc.sync.dma_start(idx4[:], offs4)
+        rd_cols = kept("rd_cols", [P, 2, 4], F32)
+        nc.sync.dma_start(out=rd_cols[:], in_=rd.rearrange("(b p t) -> p b t", b=2, t=4))
+        factor = kept("factor", [P, 4], F32)
+        with nc.allow_non_contiguous_dma(reason="one factor a partition"):
+            nc.sync.dma_start(out=factor[:], in_=gz.rearrange("(c p) -> p c", p=P))
+        load_exposure(1)
+        load_weights(1)
+        for q in (0, 2, 1, 3):
+            nc.sync.dma_start(out=wgs_rest[32 * q : 32 * q + 32, :, :], in_=wgs_rows[:, 1:4, :])
+        load_page(1)
+        for n in (2, 3):
+            load_exposure(n)
+            load_page(n)
+
+        acc, bent, plain, exposed = {}, {}, {}, {0: exposure[0]}
+
+        def psum_bank(k):
+            return psum.tile([P, 512], F32, name="bank", tag="bank%d" % k)
+
+        def open_block(jb, k):
+            acc[jb] = psum_bank(k)
+            bent[jb] = kept("bent%d" % jb, [P, 4, P], F32)
+            plain[jb] = kept("plain%d" % jb, [P, 4, P], F32)
+
+        def multiply(b, jb, a):
+            cols = slice(P * jb, P * (jb + 1))
+            if a < 2:
+                rhs = w4_codes[b][:, a, :].bitcast(FP4X4)
+                rhs_scale = w4_planes[:, a, 512 * b : 512 * (b + 1)]
+            else:
+                rhs = w1_codes[b][:].bitcast(FP8X4)
+                rhs_scale = w1_plane[b][:]
+            nc.tensor.matmul_mx(
+                out=acc[jb][:],
+                lhsT=v_codes[a][:, cols].bitcast(FP8X4),
+                lhsT_scale=v_plane[a][:, cols],
+                rhs=rhs,
+                rhs_scale=rhs_scale,
+                start=(a == 0),
+                stop=(a == 2),
+            )
+
+        def empty(jb, t0, t1):
+            dealt = acc[jb][:].rearrange("p (q t) -> p t q", t=4)[:, t0:t1, :]
+            nc.scalar.activation(out=bent[jb][:, t0:t1, :], in_=dealt, func=ACT.Gelu_apprx_tanh)
+            nc.scalar.copy(out=plain[jb][:, t0:t1, :], in_=dealt)
+
+        def turn(n, jb0, jb1, k):
+            t = n % 4
+            bank = psum_bank(k)
+            for i, jb in enumerate(range(jb0, jb1)):
+                dst = bank[:, P * i : P * (i + 1)]
+                nc.tensor.matmul(dst, lhsT=bent[jb][:, t, :], rhs=identity[:],
+                                 is_transpose=True, start=True, stop=False)
+                nc.tensor.matmul(dst, lhsT=plain[jb][:, t, :], rhs=identity[:],
+                                 is_transpose=True, start=False, stop=True)
+            return bank[:, 0 : P * (jb1 - jb0)]
+
+        def expose_on_vector(n, jb0, jb1, k):
+            cols = slice(P * jb0, P * jb1)
+            nc.vector.tensor_tensor(exposed[n][:, cols], turn(n, jb0, jb1, k), exposure[n][:, cols], ALU.mult)
+
+        def expose_on_gpsimd(n, banks):
+            summed = placed("summed%d" % n, [P, S], F32, 92 + 4 * (n % 4))
+            for half in range(2):
+                nc.scalar.copy(out=summed[:, 512 * half : 512 * (half + 1)],
+                               in_=turn(n, 4 * half, 4 * half + 4, banks[half]))
+            if MODE == "R":
+                nc.gpsimd.tensor_tensor(exposure[n][:], exposure[n][:], weight[n % 4], ALU.mult)
+            nc.gpsimd.tensor_tensor(exposure[n][:], summed[:], exposure[n][:], ALU.mult)
+
+        def produce(n, banks):
+            exposed[n] = placed("exposed1", [P, S], F32, 76) if n == 1 else exposure[n]
+            if MODE == "P" or n < 2:
+                for half in range(2):
+                    expose_on_vector(n, 4 * half, 4 * half + 4, banks[half])
+            else:
+                expose_on_gpsimd(n, banks)
+
+        def scatter(n, c0, c1):
+            window = page[n][:].indirect(idx2[:, c0 // 16 : c1 // 16])
+            if MODE == "R" and n > 1:
+                nc.vector.tensor_copy(window, exposed[n][:, c0:c1])
+            else:
+                nc.vector.tensor_tensor(window, exposed[n][:, c0:c1], weight[n % 4][:, c0:c1], ALU.mult)
+
+        x1_rows = [kept("x1_rows%d" % b, [P, 4, NP], BF16) for b in range(2)]
+        x2_rows = kept("x2_rows", [P, 4, NP], BF16)
+        x2_woven = [placed("x2_woven0", [P, 4 * NP], BF16, 56), placed("x2_woven1", [P, 4 * NP], BF16, 48)]
+
+        def fetch(n):
+            b, t = divmod(n, 4)
+            fetched = kept("fetched", [P, NP], F32, bufs=3)
+            size = placed("size%d" % n, [P, NP], F32, 92 + 4 * ((n + 2) % 4))
+            pieces = 2 if n == 7 else 1
+            width = NP // pieces
+            for i in range(pieces):
+                cols = slice(width * i, width * (i + 1))
+                nc.vector.tensor_copy(
+                    fetched[:, cols], page[n][:].indirect(idx4[:, width * i // 16 : width * (i + 1) // 16])
+                )
+                nc.scalar.activation(out=size[:, cols], in_=fetched[:, cols], func=ACT.Abs)
+                if b == 0:
+                    dst = x2_rows[:, t, cols]
+                else:
+                    dst = x2_woven[1][:].rearrange("p (c t) -> p c t", t=4)[:, cols, t]
+                nc.scalar.activation(out=dst, in_=size[:, cols], func=ACT.Copy,
+                                     scale=rd_cols[:, b, t : t + 1])
+            nc.vector.tensor_copy(x1_rows[b][:, t, :], page[n][:].indirect(idx3[:]))
+
+        score = []
+
+        def second_stage(b):
+            x1_woven = placed("x1_woven%d" % b, [P, 4 * NP], BF16, 52 if b == 0 else 60)
+            dst, src = woven(x1_woven[:], x1_rows[b][:])
+            if b == 0:
+                nc.scalar.copy(out=dst, in_=src)
+                dst, src = woven(x2_woven[0][:], x2_rows[:])
+                nc.scalar.copy(out=dst, in_=src)
+            else:
+                nc.vector.tensor_copy(dst, src)
+            codes = placed("x_codes%d" % b, [P, 2, NP], U32, 76 + 4 * b)
+            plane = kept("x_plane%d" % b, [P, 2, NP], U8)
+            nc.vector.quantize_mx(out=codes[:, 1, :].bitcast(FP8X4), scales=plane[:, 1, :], in_=x2_woven[b][:])
+            nc.vector.quantize_mx(out=codes[:, 0, :].bitcast(FP8X4), scales=plane[:, 0, :], in_=x1_woven[:])
+            for mb in range(4):
+                if b == 0:
+                    score.append(psum_bank(mb))
+                cols = slice(P * mb, P * (mb + 1))
+                nc.tensor.matmul_mx(
+                    out=score[mb][:],
+                    lhsT=codes[:, 0, cols].bitcast(FP8X4),
+                    lhsT_scale=plane[:, 0, cols],
+                    rhs=codes[:, 1, :].bitcast(FP8X4),
+                    rhs_scale=plane[:, 1, :],
+                    start=(b == 0),
+                    stop=(b == 1),
+                )
+
+        for jb in range(7):
+            open_block(jb, jb + 1)
+        for a in range(2):
+            for jb in range(7):
+                multiply(0, jb, a)
+        for piece in range(4):
+            for jb in (2 * piece, 2 * piece + 1):
+                if jb == 7:
+                    open_block(7, 1)
+                    multiply(0, 7, 0)
+                    multiply(0, 7, 1)
+                multiply(0, jb, 2)
+                empty(jb, 0, 1)
+            expose_on_vector(0, 2 * piece, 2 * piece + 2, 0)
+            scatter(0, 256 * piece, 256 * (piece + 1))
+            if piece == 0:
+                empty(0, 1, 4)
+        empty(1, 1, 4)
+        for jb in range(2, 8):
+            empty(jb, 1, 2)
+        quantize_w1(1)
+        produce(1, (0, 2))
+        for jb in range(2, 8):
+            empty(jb, 2, 4)
+        produce(2, (3, 4))
+        produce(3, (5, 6))
+        for jb in range(8):
+            open_block(jb, jb % 4)
+            for a in range(3):
+                multiply(1, jb, a)
+            empty(jb, 0, 4)
+        bound = kept("bound", [P, 4, NP], F32)
+        for n in range(8):
+            if n > 0:
+                scatter(n, 0, S)
+            for ahead in {1: (4, 5), 2: (6,), 3: (7,)}.get(n, ()):
+                load_exposure(ahead)
+                load_page(ahead)
+                produce(ahead, (4 + 2 * (ahead % 2), 5 + 2 * (ahead % 2)))
+            fetch(n)
+            if n == 3:
+                nc.sync.dma_start(out=bound[:], in_=pair.rearrange("(c p) j -> p c j", p=P))
+            if n == 4:
+                second_stage(0)
+        second_stage(1)
+        for mb in range(4):
+            result = placed("result%d" % mb, [P, NP], F32, 64 + 2 * mb)
+            pieces = 2 if mb == 3 else 1
+            width = NP // pieces
+            for i in range(pieces):
+                cols = slice(width * i, width * (i + 1))
+                nc.vector.tensor_tensor(bound[:, mb, cols], score[mb][:, cols], bound[:, mb, cols], ALU.max)
+                nc.scalar.activation(out=result[:, cols], in_=bound[:, mb, cols], func=ACT.Copy,
+                                     scale=factor[:, mb : mb + 1])
+                nc.sync.dma_start(out=out[P * mb : P * (mb + 1), cols], in_=result[:, cols])

@@ -19,6 +19,8 @@ ALU = mybir.AluOpType
 
 P = 128
 KB = 1024
+EXPOSURE_KB = (8, 24, 40, 68)
+PAGE_KB = (0, 16, 60)
 MODE = "Q"
 
 
@@ -51,16 +53,17 @@ def tile_list_gauze_ageing_match_kernel(
         idx3 = lists.tile([P, NP // 16], U16, name="idx3")
         idx4 = lists.tile([P, NP // 16], U16, name="idx4")
 
-        scale_window = placed("scale_window", [P, T], U8, 70)
-        nc.vector.memset(scale_window[:].bitcast(I32), 0)
+        scale_window = placed("scale_window", [P, T], U8, 46)
+        for q in range(4):
+            nc.vector.memset(scale_window[32 * q : 32 * q + 20, :].bitcast(I32), 0)
         w4_planes = kept("w4_planes", [P, 2, H], U8)
-        shifted_scales = kept("shifted_scales", [P, S], U8)
+        shifted_scales = kept("shifted_scales", [P, 2, S], U8)
 
         nc.sync.dma_start(idx[:], offs)
 
         for q in range(4):
-            nc.gpsimd.dma_start(
-                out=scale_window[32 * q : 32 * q + 12, :].bitcast(I32),
+            (nc.scalar if q == 0 else nc.gpsimd).dma_start(
+                out=scale_window[32 * q + 20 : 32 * q + 32, :].bitcast(I32),
                 in_=tab_scales[:, 4 * q : 4 * q + 4, :].bitcast(I32),
             )
         table = [placed("table%d" % a, [P, T], I32, 16 * a) for a in range(3)]
@@ -70,24 +73,28 @@ def tile_list_gauze_ageing_match_kernel(
                 out=table[a][:], in_=tab_words[a].rearrange("p n i -> p (n i)").bitcast(I32)
             )
 
-        w4_codes = [kept("w4_codes%d" % b, [P, 2, 2 * 512], U8) for b in range(2)]
+        w4_codes = {}
         w1_codes = [kept("w1_codes%d" % b, [P, 512], U32) for b in range(2)]
         w1_plane = [kept("w1_plane%d" % b, [P, 512], U8) for b in range(2)]
         w1_raw = {}
 
         def load_weights(b):
+            if b == 0:
+                w4_codes[b] = kept("w4_codes0", [P, 2, 2 * 512], U8)
+            else:
+                w4_codes[b] = placed("w4_codes1", [P, 2, 2 * 512], U8, 44)
             nc.sync.dma_start(
                 out=w4_codes[b][:].bitcast(I32),
                 in_=w4_words.rearrange("a p c -> p a c")[:, :, 1024 * b : 1024 * (b + 1)].bitcast(I32),
             )
-            w1_raw[b] = placed("w1_raw%d" % b, [P, 4, 512], F32, 52)
+            w1_raw[b] = placed("w1_raw%d" % b, [P, 4, 512], F32, 60)
             nc.sync.dma_start(
                 out=w1_raw[b][:],
                 in_=w1[:, 512 * b : 512 * (b + 1)].rearrange("(p i) c -> p i c", i=4),
             )
 
         def quantize_w1(b):
-            rounded = placed("w1_rounded%d" % b, [P, 2048], BF16, 60 if b == 0 else 76)
+            rounded = placed("w1_rounded%d" % b, [P, 2048], BF16, 68 if b == 0 else EXPOSURE_KB[0])
             dst, src = woven(rounded[:], w1_raw[b][:])
             nc.scalar.copy(out=dst, in_=src)
             nc.vector.quantize_mx(
@@ -103,18 +110,22 @@ def tile_list_gauze_ageing_match_kernel(
             )
         nc.sync.dma_start(idx2[:], offs2)
         load_table(1)
-        load_table(2)
+        nc.sync.dma_start(idx3[:], offs3)
+        nc.sync.dma_start(idx4[:], offs4)
 
         picked_scales = kept("picked_scales", [P, S], U8)
         nc.vector.tensor_copy(picked_scales[:], scale_window[:].indirect(idx[:]))
-        nc.gpsimd.dma_start(
-            out=shifted_scales[0:112, :].bitcast(I32), in_=picked_scales[4:116, :].bitcast(I32)
-        )
-        v_plane = [picked_scales[:], shifted_scales[:], picked_scales[8:P, :]]
+        for a in range(2):
+            nc.sync.dma_start(
+                out=shifted_scales[0 : 108 - 4 * a, a, :].bitcast(I32),
+                in_=picked_scales[20 + 4 * a : P, :].bitcast(I32),
+            )
+        load_table(2)
+        v_plane = [shifted_scales[:, 0, :], shifted_scales[:, 1, :], shifted_scales[8:P, 0, :]]
         identity = kept("identity", [P, P], F32)
         make_identity(nc, identity[:])
 
-        v_codes = [placed("v_codes%d" % a, [P, S], U32, 64 + 4 * a) for a in range(3)]
+        v_codes = [placed("v_codes%d" % a, [P, S], U32, 48 + 4 * a) for a in range(3)]
         nc.vector.tensor_copy(v_codes[0][:], table[0][:].bitcast(U32).indirect(idx[:]))
         quantize_w1(0)
         nc.vector.tensor_copy(v_codes[1][:], table[1][:].bitcast(U32).indirect(idx[:]))
@@ -130,43 +141,45 @@ def tile_list_gauze_ageing_match_kernel(
             b, t = divmod(n, 4)
             return x[512 * b : 512 * (b + 1), :].rearrange("(p t) j -> p t j", t=4)[:, t, :]
 
-        def load_exposure(n):
-            exposure[n] = placed("exposure%d" % n, [P, S], F32, 76 + 4 * (n % 4))
-            nc.sync.dma_start(out=exposure[n][:], in_=rows_of(ex, n))
+        def load_exposure(n, c0=0, c1=S):
+            if c0 == 0:
+                exposure[n] = placed("exposure%d" % n, [P, S], F32, EXPOSURE_KB[n % 4])
+            nc.sync.dma_start(out=exposure[n][:, c0:c1], in_=rows_of(ex, n)[:, c0:c1])
 
         def load_page(n):
-            if n < 2:
-                page[n] = kept("page%d" % n, [P, T2], F32)
-            else:
-                page[n] = placed("page%d" % n, [P, T2], F32, 8 * (n - 2))
+            page[n] = placed("page%d" % n, [P, T2], F32, PAGE_KB[n % 3])
             nc.sync.dma_start(out=page[n][:], in_=rows_of(page0, n))
 
-        wgs_first = kept("wgs_first", [P, S], F32)
-        wgs_rest = kept("wgs_rest", [P, 3, S], F32)
         wgs_rows = wgs.rearrange("(q t) j -> q t j", t=4)
-        weight = [wgs_first[:]] + [wgs_rest[:, t, :] for t in range(3)]
+        wgs_tiles = {
+            0: placed("wgs0", [P, 1, S], F32, 12),
+            1: placed("wgs1", [P, 1, S], F32, 28),
+            2: placed("wgs23", [P, 2, S], F32, 32),
+        }
+        weight = [wgs_tiles[0][:, 0, :], wgs_tiles[1][:, 0, :], wgs_tiles[2][:, 0, :], wgs_tiles[2][:, 1, :]]
 
-        load_exposure(0)
-        for q in (0, 2, 1, 3):
-            nc.sync.dma_start(out=wgs_first[32 * q : 32 * q + 32, :], in_=wgs_rows[:, 0, :])
+        def load_wgs(t0, t1, c0=0, c1=S):
+            for q in (0, 2, 1, 3):
+                nc.sync.dma_start(
+                    out=wgs_tiles[t0][32 * q : 32 * q + 32, :, c0:c1], in_=wgs_rows[:, t0:t1, c0:c1]
+                )
+
+        load_exposure(0, 0, 512)
+        load_wgs(0, 1, 0, 512)
         load_page(0)
-        nc.sync.dma_start(idx3[:], offs3)
-        nc.sync.dma_start(idx4[:], offs4)
-        rd_cols = kept("rd_cols", [P, 2, 4], F32)
-        nc.sync.dma_start(out=rd_cols[:], in_=rd.rearrange("(b p t) -> p b t", b=2, t=4))
-        factor = kept("factor", [P, 4], F32)
-        with nc.allow_non_contiguous_dma(reason="one factor a partition"):
-            nc.sync.dma_start(out=factor[:], in_=gz.rearrange("(c p) -> p c", p=P))
+        load_exposure(0, 512, S)
+        load_wgs(0, 1, 512, S)
         load_exposure(1)
         load_weights(1)
-        for q in (0, 2, 1, 3):
-            nc.sync.dma_start(out=wgs_rest[32 * q : 32 * q + 32, :, :], in_=wgs_rows[:, 1:4, :])
+        load_wgs(1, 2)
         load_page(1)
-        for n in (2, 3):
-            load_exposure(n)
-            load_page(n)
+        load_exposure(2)
+        rd_cols = placed("rd_cols", [P, 2, 4], F32, 46)
+        nc.sync.dma_start(out=rd_cols[:], in_=rd.rearrange("(b p t) -> p b t", b=2, t=4))
+        load_wgs(2, 4)
+        load_exposure(3)
 
-        acc, bent, plain, exposed = {}, {}, {}, {0: exposure[0]}
+        acc, bent, plain = {}, {}, {}
 
         def psum_bank(k):
             return psum.tile([P, 512], F32, name="bank", tag="bank%d" % k)
@@ -212,40 +225,28 @@ def tile_list_gauze_ageing_match_kernel(
 
         def expose_on_vector(n, jb0, jb1, k):
             cols = slice(P * jb0, P * jb1)
-            nc.vector.tensor_tensor(exposed[n][:, cols], turn(n, jb0, jb1, k), exposure[n][:, cols], ALU.mult)
-
-        def expose_on_gpsimd(n, banks):
-            summed = placed("summed%d" % n, [P, S], F32, 92 + 4 * (n % 4))
-            for half in range(2):
-                nc.scalar.copy(out=summed[:, 512 * half : 512 * (half + 1)],
-                               in_=turn(n, 4 * half, 4 * half + 4, banks[half]))
-            if MODE == "R":
-                nc.gpsimd.tensor_tensor(exposure[n][:], exposure[n][:], weight[n % 4], ALU.mult)
-            nc.gpsimd.tensor_tensor(exposure[n][:], summed[:], exposure[n][:], ALU.mult)
+            nc.vector.tensor_tensor(exposure[n][:, cols], turn(n, jb0, jb1, k), exposure[n][:, cols], ALU.mult)
 
         def produce(n, banks):
-            exposed[n] = placed("exposed1", [P, S], F32, 76) if n == 1 else exposure[n]
-            if MODE == "P" or n < 2:
-                for half in range(2):
-                    expose_on_vector(n, 4 * half, 4 * half + 4, banks[half])
-            else:
-                expose_on_gpsimd(n, banks)
+            summed = placed("summed%d" % n, [P, S], F32, 72 + 4 * (n % 4))
+            for half in range(2):
+                cols = slice(512 * half, 512 * (half + 1))
+                nc.scalar.copy(out=summed[:, cols], in_=turn(n, 4 * half, 4 * half + 4, banks[half]))
+                nc.gpsimd.tensor_tensor(exposure[n][:, cols], summed[:, cols], exposure[n][:, cols], ALU.mult)
 
         def scatter(n, c0, c1):
             window = page[n][:].indirect(idx2[:, c0 // 16 : c1 // 16])
-            if MODE == "R" and n > 1:
-                nc.vector.tensor_copy(window, exposed[n][:, c0:c1])
-            else:
-                nc.vector.tensor_tensor(window, exposed[n][:, c0:c1], weight[n % 4][:, c0:c1], ALU.mult)
+            nc.vector.tensor_tensor(window, exposure[n][:, c0:c1], weight[n % 4][:, c0:c1], ALU.mult)
 
-        x1_rows = [kept("x1_rows%d" % b, [P, 4, NP], BF16) for b in range(2)]
+        x1_rows = [kept("x1_rows0", [P, 4, NP], BF16), kept("x1_rows1", [P, 2, NP], BF16)]
+        x1_woven = [kept("x1_woven%d" % b, [P, 4 * NP], BF16) for b in range(2)]
         x2_rows = kept("x2_rows", [P, 4, NP], BF16)
-        x2_woven = [placed("x2_woven0", [P, 4 * NP], BF16, 56), placed("x2_woven1", [P, 4 * NP], BF16, 48)]
+        x2_woven = [kept("x2_woven%d" % b, [P, 4 * NP], BF16) for b in range(2)]
 
         def fetch(n):
             b, t = divmod(n, 4)
             fetched = kept("fetched", [P, NP], F32, bufs=3)
-            size = placed("size%d" % n, [P, NP], F32, 92 + 4 * ((n + 2) % 4))
+            size = placed("size%d" % n, [P, NP], F32, 72 + 4 * ((n + 2) % 4))
             pieces = 2 if n == 7 else 1
             width = NP // pieces
             for i in range(pieces):
@@ -260,23 +261,36 @@ def tile_list_gauze_ageing_match_kernel(
                     dst = x2_woven[1][:].rearrange("p (c t) -> p c t", t=4)[:, cols, t]
                 nc.scalar.activation(out=dst, in_=size[:, cols], func=ACT.Copy,
                                      scale=rd_cols[:, b, t : t + 1])
-            nc.vector.tensor_copy(x1_rows[b][:, t, :], page[n][:].indirect(idx3[:]))
+            if n < 6:
+                dst = x1_rows[b][:, t, :]
+            else:
+                dst = x1_woven[1][:].rearrange("p (c t) -> p c t", t=4)[:, :, t]
+            nc.vector.tensor_copy(dst, page[n][:].indirect(idx3[:]))
+            if n == 5:
+                nc.scalar.copy(
+                    out=x1_woven[1][:].rearrange("p (c t) -> p c t", t=4)[:, :, 0:2],
+                    in_=x1_rows[1][:].rearrange("p t c -> p c t"),
+                )
 
         score = []
 
         def second_stage(b):
-            x1_woven = placed("x1_woven%d" % b, [P, 4 * NP], BF16, 52 if b == 0 else 60)
-            dst, src = woven(x1_woven[:], x1_rows[b][:])
             if b == 0:
-                nc.scalar.copy(out=dst, in_=src)
-                dst, src = woven(x2_woven[0][:], x2_rows[:])
-                nc.scalar.copy(out=dst, in_=src)
-            else:
-                nc.vector.tensor_copy(dst, src)
-            codes = placed("x_codes%d" % b, [P, 2, NP], U32, 76 + 4 * b)
+                for target, rows in ((x1_woven[0], x1_rows[0]), (x2_woven[0], x2_rows)):
+                    dst, src = woven(target[:], rows[:])
+                    nc.scalar.copy(out=dst, in_=src)
+            codes = placed("x_codes%d" % b, [P, 2, NP], U32, EXPOSURE_KB[b])
             plane = kept("x_plane%d" % b, [P, 2, NP], U8)
             nc.vector.quantize_mx(out=codes[:, 1, :].bitcast(FP8X4), scales=plane[:, 1, :], in_=x2_woven[b][:])
-            nc.vector.quantize_mx(out=codes[:, 0, :].bitcast(FP8X4), scales=plane[:, 0, :], in_=x1_woven[:])
+            pieces = 1 + b
+            width = NP // pieces
+            for i in range(pieces):
+                cols = slice(width * i, width * (i + 1))
+                nc.vector.quantize_mx(
+                    out=codes[:, 0, cols].bitcast(FP8X4),
+                    scales=plane[:, 0, cols],
+                    in_=x1_woven[b][:, 4 * width * i : 4 * width * (i + 1)],
+                )
             for mb in range(4):
                 if b == 0:
                     score.append(psum_bank(mb))
@@ -311,8 +325,9 @@ def tile_list_gauze_ageing_match_kernel(
         empty(1, 1, 4)
         for jb in range(2, 8):
             empty(jb, 1, 2)
-        quantize_w1(1)
         produce(1, (0, 2))
+        quantize_w1(1)
+        load_page(2)
         for jb in range(2, 8):
             empty(jb, 2, 4)
         produce(2, (3, 4))
@@ -322,22 +337,27 @@ def tile_list_gauze_ageing_match_kernel(
             for a in range(3):
                 multiply(1, jb, a)
             empty(jb, 0, 4)
-        bound = kept("bound", [P, 4, NP], F32)
+        bound = placed("bound", [P, 4, NP], F32, 48)
         for n in range(8):
             if n > 0:
                 scatter(n, 0, S)
-            for ahead in {1: (4, 5), 2: (6,), 3: (7,)}.get(n, ()):
+            if n + 4 < 8:
+                ahead = n + 4
                 load_exposure(ahead)
-                load_page(ahead)
                 produce(ahead, (4 + 2 * (ahead % 2), 5 + 2 * (ahead % 2)))
             fetch(n)
+            if n + 3 < 8:
+                load_page(n + 3)
             if n == 3:
                 nc.sync.dma_start(out=bound[:], in_=pair.rearrange("(c p) j -> p c j", p=P))
+                factor = placed("factor", [P, 4], F32, 56)
+                with nc.allow_non_contiguous_dma(reason="one factor a partition"):
+                    nc.sync.dma_start(out=factor[:], in_=gz.rearrange("(c p) -> p c", p=P))
             if n == 4:
                 second_stage(0)
         second_stage(1)
         for mb in range(4):
-            result = placed("result%d" % mb, [P, NP], F32, 64 + 2 * mb)
+            result = kept("result%d" % mb, [P, NP], F32)
             pieces = 2 if mb == 3 else 1
             width = NP // pieces
             for i in range(pieces):

from contextlib import ExitStack

import concourse.mybir as mybir
from concourse.masks import make_identity

K, KA, H, T, S, T2, NP = 1536, 1024, 1024, 4096, 1024, 2048, 512
FLOPS = 2 * K * H * S + 2 * H * NP * NP

F32 = mybir.dt.float32
BF16 = mybir.dt.bfloat16
I32 = mybir.dt.int32
U32 = mybir.dt.uint32
U16 = mybir.dt.uint16
U8 = mybir.dt.uint8
FP8X4 = mybir.dt.float8_e4m3fn_x4
FP4X4 = mybir.dt.float4_e2m1fn_x4
ACT = mybir.ActivationFunctionType
ALU = mybir.AluOpType

P = 128
KB = 1024
EXPOSURE_KB = (8, 24, 40, 68)
PAGE_KB = (0, 16, 60)
MODE = "Q"


def woven(dst, src):
    return (
        dst.rearrange("p (c i t) -> p c t i", i=4, t=4),
        src.rearrange("p t (c i) -> p c t i", i=4),
    )


def tile_list_gauze_ageing_match_kernel(
    tc, tab_words, tab_scales, w4_words, w4_scales, w1, ex, page0, wgs, rd, pair, gz,
    offs, offs2, offs3, offs4, out,
):
    nc = tc.nc
    with ExitStack() as ctx:
        lists = ctx.enter_context(tc.tile_pool(name="lists", bufs=1))
        keep = ctx.enter_context(tc.tile_pool(name="keep", bufs=1))
        shared = ctx.enter_context(tc.tile_pool(name="shared", bufs=1))
        psum = ctx.enter_context(tc.psum_pool(name="psum", bufs=1))

        def placed(name, shape, dtype, kb):
            return shared.tile(shape, dtype, name=name, offset=kb * KB, align_bytes=64)

        def kept(name, shape, dtype, bufs=1):
            return keep.tile(shape, dtype, name=name, bufs=bufs, align_bytes=64)

        idx = lists.tile([P, S // 16], U16, name="idx")
        idx2 = lists.tile([P, S // 16], U16, name="idx2")
        idx3 = lists.tile([P, NP // 16], U16, name="idx3")
        idx4 = lists.tile([P, NP // 16], U16, name="idx4")

        scale_window = placed("scale_window", [P, T], U8, 46)
        for q in range(4):
            nc.vector.memset(scale_window[32 * q : 32 * q + 20, :].bitcast(I32), 0)
        w4_planes = kept("w4_planes", [P, 2, H], U8)
        shifted_scales = kept("shifted_scales", [P, 2, S], U8)

        nc.sync.dma_start(idx[:], offs)

        for q in range(4):
            (nc.scalar if q == 0 else nc.gpsimd).dma_start(
                out=scale_window[32 * q + 20 : 32 * q + 32, :].bitcast(I32),
                in_=tab_scales[:, 4 * q : 4 * q + 4, :].bitcast(I32),
            )
        table = [placed("table%d" % a, [P, T], I32, 16 * a) for a in range(3)]

        def load_table(a):
            nc.sync.dma_start(
                out=table[a][:], in_=tab_words[a].rearrange("p n i -> p (n i)").bitcast(I32)
            )

        w4_codes = {}
        w1_codes = [kept("w1_codes%d" % b, [P, 512], U32) for b in range(2)]
        w1_plane = [kept("w1_plane%d" % b, [P, 512], U8) for b in range(2)]
        w1_raw = {}

        def load_weights(b):
            if b == 0:
                w4_codes[b] = kept("w4_codes0", [P, 2, 2 * 512], U8)
            else:
                w4_codes[b] = placed("w4_codes1", [P, 2, 2 * 512], U8, 44)
            nc.sync.dma_start(
                out=w4_codes[b][:].bitcast(I32),
                in_=w4_words.rearrange("a p c -> p a c")[:, :, 1024 * b : 1024 * (b + 1)].bitcast(I32),
            )
            w1_raw[b] = placed("w1_raw%d" % b, [P, 4, 512], F32, 60)
            nc.sync.dma_start(
                out=w1_raw[b][:],
                in_=w1[:, 512 * b : 512 * (b + 1)].rearrange("(p i) c -> p i c", i=4),
            )

        def quantize_w1(b):
            rounded = placed("w1_rounded%d" % b, [P, 2048], BF16, 68 if b == 0 else EXPOSURE_KB[0])
            dst, src = woven(rounded[:], w1_raw[b][:])
            nc.scalar.copy(out=dst, in_=src)
            nc.vector.quantize_mx(
                out=w1_codes[b][:].bitcast(FP8X4), scales=w1_plane[b][:], in_=rounded[:]
            )

        load_table(0)
        load_weights(0)
        for q in range(4):
            nc.sync.dma_start(
                out=w4_planes[32 * q : 32 * q + 4, :, :].bitcast(I32),
                in_=w4_scales[:, 4 * q : 4 * q + 4, :].rearrange("a r c -> r a c").bitcast(I32),
            )
        nc.sync.dma_start(idx2[:], offs2)
        load_table(1)
        nc.sync.dma_start(idx3[:], offs3)
        nc.sync.dma_start(idx4[:], offs4)

        picked_scales = kept("picked_scales", [P, S], U8)
        nc.vector.tensor_copy(picked_scales[:], scale_window[:].indirect(idx[:]))
        for a in range(2):
            nc.sync.dma_start(
                out=shifted_scales[0 : 108 - 4 * a, a, :].bitcast(I32),
                in_=picked_scales[20 + 4 * a : P, :].bitcast(I32),
            )
        load_table(2)
        v_plane = [shifted_scales[:, 0, :], shifted_scales[:, 1, :], shifted_scales[8:P, 0, :]]
        identity = kept("identity", [P, P], F32)
        make_identity(nc, identity[:])

        v_codes = [placed("v_codes%d" % a, [P, S], U32, 48 + 4 * a) for a in range(3)]
        nc.vector.tensor_copy(v_codes[0][:], table[0][:].bitcast(U32).indirect(idx[:]))
        quantize_w1(0)
        nc.vector.tensor_copy(v_codes[1][:], table[1][:].bitcast(U32).indirect(idx[:]))
        for half in range(2):
            nc.vector.tensor_copy(
                v_codes[2][:, 512 * half : 512 * (half + 1)],
                table[2][:].bitcast(U32).indirect(idx[:, 32 * half : 32 * (half + 1)]),
            )

        exposure, page = {}, {}

        def rows_of(x, n):
            b, t = divmod(n, 4)
            return x[512 * b : 512 * (b + 1), :].rearrange("(p t) j -> p t j", t=4)[:, t, :]

        def load_exposure(n, c0=0, c1=S):
            if c0 == 0:
                exposure[n] = placed("exposure%d" % n, [P, S], F32, EXPOSURE_KB[n % 4])
            nc.sync.dma_start(out=exposure[n][:, c0:c1], in_=rows_of(ex, n)[:, c0:c1])

        def load_page(n):
            page[n] = placed("page%d" % n, [P, T2], F32, PAGE_KB[n % 3])
            nc.sync.dma_start(out=page[n][:], in_=rows_of(page0, n))

        wgs_rows = wgs.rearrange("(q t) j -> q t j", t=4)
        wgs_tiles = {
            0: placed("wgs0", [P, 1, S], F32, 12),
            1: placed("wgs1", [P, 1, S], F32, 28),
            2: placed("wgs23", [P, 2, S], F32, 32),
        }
        weight = [wgs_tiles[0][:, 0, :], wgs_tiles[1][:, 0, :], wgs_tiles[2][:, 0, :], wgs_tiles[2][:, 1, :]]

        def load_wgs(t0, t1, c0=0, c1=S):
            for q in (0, 2, 1, 3):
                nc.sync.dma_start(
                    out=wgs_tiles[t0][32 * q : 32 * q + 32, :, c0:c1], in_=wgs_rows[:, t0:t1, c0:c1]
                )

        load_exposure(0, 0, 512)
        load_wgs(0, 1, 0, 512)
        load_page(0)
        load_exposure(0, 512, S)
        load_wgs(0, 1, 512, S)
        load_exposure(1)
        load_weights(1)
        load_wgs(1, 2)
        load_page(1)
        load_exposure(2)
        rd_cols = placed("rd_cols", [P, 2, 4], F32, 46)
        nc.sync.dma_start(out=rd_cols[:], in_=rd.rearrange("(b p t) -> p b t", b=2, t=4))
        load_wgs(2, 4)
        load_exposure(3)

        acc, bent, plain = {}, {}, {}

        def psum_bank(k):
            return psum.tile([P, 512], F32, name="bank", tag="bank%d" % k)

        def open_block(jb, k):
            acc[jb] = psum_bank(k)
            bent[jb] = kept("bent%d" % jb, [P, 4, P], F32)
            plain[jb] = kept("plain%d" % jb, [P, 4, P], F32)

        def multiply(b, jb, a):
            cols = slice(P * jb, P * (jb + 1))
            if a < 2:
                rhs = w4_codes[b][:, a, :].bitcast(FP4X4)
                rhs_scale = w4_planes[:, a, 512 * b : 512 * (b + 1)]
            else:
                rhs = w1_codes[b][:].bitcast(FP8X4)
                rhs_scale = w1_plane[b][:]
            nc.tensor.matmul_mx(
                out=acc[jb][:],
                lhsT=v_codes[a][:, cols].bitcast(FP8X4),
                lhsT_scale=v_plane[a][:, cols],
                rhs=rhs,
                rhs_scale=rhs_scale,
                start=(a == 0),
                stop=(a == 2),
            )

        def empty(jb, t0, t1):
            dealt = acc[jb][:].rearrange("p (q t) -> p t q", t=4)[:, t0:t1, :]
            nc.scalar.activation(out=bent[jb][:, t0:t1, :], in_=dealt, func=ACT.Gelu_apprx_tanh)
            nc.scalar.copy(out=plain[jb][:, t0:t1, :], in_=dealt)

        def turn(n, jb0, jb1, k):
            t = n % 4
            bank = psum_bank(k)
            for i, jb in enumerate(range(jb0, jb1)):
                dst = bank[:, P * i : P * (i + 1)]
                nc.tensor.matmul(dst, lhsT=bent[jb][:, t, :], rhs=identity[:],
                                 is_transpose=True, start=True, stop=False)
                nc.tensor.matmul(dst, lhsT=plain[jb][:, t, :], rhs=identity[:],
                                 is_transpose=True, start=False, stop=True)
            return bank[:, 0 : P * (jb1 - jb0)]

        def expose_on_vector(n, jb0, jb1, k):
            cols = slice(P * jb0, P * jb1)
            nc.vector.tensor_tensor(exposure[n][:, cols], turn(n, jb0, jb1, k), exposure[n][:, cols], ALU.mult)

        def produce(n, banks):
            summed = placed("summed%d" % n, [P, S], F32, 72 + 4 * (n % 4))
            for half in range(2):
                cols = slice(512 * half, 512 * (half + 1))
                nc.scalar.copy(out=summed[:, cols], in_=turn(n, 4 * half, 4 * half + 4, banks[half]))
                nc.gpsimd.tensor_tensor(exposure[n][:, cols], summed[:, cols], exposure[n][:, cols], ALU.mult)

        def scatter(n, c0, c1):
            window = page[n][:].indirect(idx2[:, c0 // 16 : c1 // 16])
            nc.vector.tensor_tensor(window, exposure[n][:, c0:c1], weight[n % 4][:, c0:c1], ALU.mult)

        x1_rows = [kept("x1_rows0", [P, 4, NP], BF16), kept("x1_rows1", [P, 2, NP], BF16)]
        x1_woven = [kept("x1_woven%d" % b, [P, 4 * NP], BF16) for b in range(2)]
        x2_rows = kept("x2_rows", [P, 4, NP], BF16)
        x2_woven = [kept("x2_woven%d" % b, [P, 4 * NP], BF16) for b in range(2)]

        def fetch(n):
            b, t = divmod(n, 4)
            fetched = kept("fetched", [P, NP], F32, bufs=3)
            size = placed("size%d" % n, [P, NP], F32, 72 + 4 * ((n + 2) % 4))
            pieces = 2 if n == 7 else 1
            width = NP // pieces
            for i in range(pieces):
                cols = slice(width * i, width * (i + 1))
                nc.vector.tensor_copy(
                    fetched[:, cols], page[n][:].indirect(idx4[:, width * i // 16 : width * (i + 1) // 16])
                )
                nc.scalar.activation(out=size[:, cols], in_=fetched[:, cols], func=ACT.Abs)
                if b == 0:
                    dst = x2_rows[:, t, cols]
                else:
                    dst = x2_woven[1][:].rearrange("p (c t) -> p c t", t=4)[:, cols, t]
                nc.scalar.activation(out=dst, in_=size[:, cols], func=ACT.Copy,
                                     scale=rd_cols[:, b, t : t + 1])
            if n < 6:
                dst = x1_rows[b][:, t, :]
            else:
                dst = x1_woven[1][:].rearrange("p (c t) -> p c t", t=4)[:, :, t]
            nc.vector.tensor_copy(dst, page[n][:].indirect(idx3[:]))
            if n == 5:
                nc.scalar.copy(
                    out=x1_woven[1][:].rearrange("p (c t) -> p c t", t=4)[:, :, 0:2],
                    in_=x1_rows[1][:].rearrange("p t c -> p c t"),
                )

        score = []

        def second_stage(b):
            if b == 0:
                for target, rows in ((x1_woven[0], x1_rows[0]), (x2_woven[0], x2_rows)):
                    dst, src = woven(target[:], rows[:])
                    nc.scalar.copy(out=dst, in_=src)
            codes = placed("x_codes%d" % b, [P, 2, NP], U32, EXPOSURE_KB[b])
            plane = kept("x_plane%d" % b, [P, 2, NP], U8)
            nc.vector.quantize_mx(out=codes[:, 1, :].bitcast(FP8X4), scales=plane[:, 1, :], in_=x2_woven[b][:])
            pieces = 1 + b
            width = NP // pieces
            for i in range(pieces):
                cols = slice(width * i, width * (i + 1))
                nc.vector.quantize_mx(
                    out=codes[:, 0, cols].bitcast(FP8X4),
                    scales=plane[:, 0, cols],
                    in_=x1_woven[b][:, 4 * width * i : 4 * width * (i + 1)],
                )
            for mb in range(4):
                if b == 0:
                    score.append(psum_bank(mb))
                cols = slice(P * mb, P * (mb + 1))
                nc.tensor.matmul_mx(
                    out=score[mb][:],
                    lhsT=codes[:, 0, cols].bitcast(FP8X4),
                    lhsT_scale=plane[:, 0, cols],
                    rhs=codes[:, 1, :].bitcast(FP8X4),
                    rhs_scale=plane[:, 1, :],
                    start=(b == 0),
                    stop=(b == 1),
                )

        for jb in range(7):
            open_block(jb, jb + 1)
        for a in range(2):
            for jb in range(7):
                multiply(0, jb, a)
        for piece in range(4):
            for jb in (2 * piece, 2 * piece + 1):
                if jb == 7:
                    open_block(7, 1)
                    multiply(0, 7, 0)
                    multiply(0, 7, 1)
                multiply(0, jb, 2)
                empty(jb, 0, 1)
            expose_on_vector(0, 2 * piece, 2 * piece + 2, 0)
            scatter(0, 256 * piece, 256 * (piece + 1))
            if piece == 0:
                empty(0, 1, 4)
        empty(1, 1, 4)
        for jb in range(2, 8):
            empty(jb, 1, 2)
        produce(1, (0, 2))
        quantize_w1(1)
        load_page(2)
        for jb in range(2, 8):
            empty(jb, 2, 4)
        produce(2, (3, 4))
        produce(3, (5, 6))
        for jb in range(8):
            open_block(jb, jb % 4)
            for a in range(3):
                multiply(1, jb, a)
            empty(jb, 0, 4)
        bound = placed("bound", [P, 4, NP], F32, 48)
        for n in range(8):
            if n > 0:
                scatter(n, 0, S)
            if n + 4 < 8:
                ahead = n + 4
                load_exposure(ahead)
                produce(ahead, (4 + 2 * (ahead % 2), 5 + 2 * (ahead % 2)))
            fetch(n)
            if n + 3 < 8:
                load_page(n + 3)
            if n == 3:
                nc.sync.dma_start(out=bound[:], in_=pair.rearrange("(c p) j -> p c j", p=P))
                factor = placed("factor", [P, 4], F32, 56)
                with nc.allow_non_contiguous_dma(reason="one factor a partition"):
                    nc.sync.dma_start(out=factor[:], in_=gz.rearrange("(c p) -> p c", p=P))
            if n == 4:
                second_stage(0)
        second_stage(1)
        for mb in range(4):
            result = kept("result%d" % mb, [P, NP], F32)
            pieces = 2 if mb == 3 else 1
            width = NP // pieces
            for i in range(pieces):
                cols = slice(width * i, width * (i + 1))
                nc.vector.tensor_tensor(bound[:, mb, cols], score[mb][:, cols], bound[:, mb, cols], ALU.max)
                nc.scalar.activation(out=result[:, cols], in_=bound[:, mb, cols], func=ACT.Copy,
                                     scale=factor[:, mb : mb + 1])
                nc.sync.dma_start(out=out[P * mb : P * (mb + 1), cols], in_=result[:, cols])
